import numpy as np
import ml_dtypes


def mxq(x, axis, fmt="e4m3"):
    dtype, down = {"e4m3": (ml_dtypes.float8_e4m3fn, 7), "e5m2": (ml_dtypes.float8_e5m2, 14)}[fmt]
    v = np.moveaxis(np.asarray(x, np.float32).astype(ml_dtypes.bfloat16).astype(np.float64), axis, -1)
    blocks = v.reshape(v.shape[:-1] + (-1, 32))
    amax = np.abs(blocks).max(-1, keepdims=True)
    byte = np.maximum(np.where(amax > 0, np.frexp(amax)[1] - 1 + 127, 0) - down, 1)
    scale = np.exp2(byte - 127.0)
    codes = (blocks / scale).astype(np.float32).astype(dtype).astype(np.float64)
    return np.moveaxis((codes * scale).reshape(v.shape), -1, axis)


WIDE = False


def mx_kscale(k):
    if not WIDE:
        return np.ones(k)
    levels = np.array([10, -10, 5, -5, 0])
    if k % 512:
        return np.exp2(np.random.permutation(np.resize(levels, k // 32))).repeat(32)
    a = np.empty((k // 512, 16))
    for p in range(k // 512):
        a[p, :8] = np.random.permutation(np.resize(levels, 8))
        for g in range(8):
            far = levels[np.abs(levels - a[p, g]) >= 10]
            a[p, g + 8] = far[np.random.randint(len(far))]
    return np.exp2(a.ravel()).repeat(32)


def f64(x):
    return np.asarray(x).astype(np.float64)


def striped(idx):
    return np.tile(np.asarray(idx).reshape(-1, 16).T, (8, 1)).astype(np.uint16)


def unstriped(offs):
    return offs[:16].T.reshape(-1).astype(np.int64)


E2M1 = np.array([0.0, 0.5, 1.0, 1.5, 2.0, 3.0, 4.0, 6.0, -0.0, -0.5, -1.0, -1.5, -2.0, -3.0, -4.0, -6.0])


def pack_weight(w, fmt):
    k, n = w.shape
    w = f64(np.asarray(w, np.float32).astype(ml_dtypes.bfloat16)).reshape(k // 32, 32, n)
    amax = np.abs(w).max(1)
    if fmt == "e4m3":
        byte = np.frexp(amax)[1] - 1 + 127 - 7
    else:
        mant, ex = np.frexp(amax / 6.0)
        byte = np.where(mant > 0.5, ex, ex - 1) + 127
    byte = np.clip(np.where(amax > 0, byte, 1), 1, 254)
    scaled = (w * np.exp2(127.0 - byte)[:, None, :]).reshape(k, n).astype(np.float32)
    by_word = np.ascontiguousarray(scaled.reshape(k // 512, 128, 4, n).transpose(0, 1, 3, 2))
    if fmt == "e4m3":
        words = by_word.astype(ml_dtypes.float8_e4m3fn).view(np.uint8)
    else:
        c = by_word.astype(ml_dtypes.float4_e2m1fn).view(np.uint8) & 0xF
        words = (c[..., 0::2] | (c[..., 1::2] << 4)).reshape(k // 512, 128, 2 * n)
    return np.ascontiguousarray(words), np.ascontiguousarray(byte.astype(np.uint8).reshape(k // 512, 16, n))


def unpack_weight(words, scales, fmt):
    g, _, n = scales.shape
    words = np.ascontiguousarray(words).reshape(g, 128, n, -1)
    if fmt == "e4m3":
        vals = words.view(ml_dtypes.float8_e4m3fn).astype(np.float64)
    else:
        nib = np.empty((g, 128, n, 4), np.uint8)
        nib[..., 0::2] = words & 0xF
        nib[..., 1::2] = words >> 4
        vals = E2M1[nib]
    vals = vals * np.repeat(np.exp2(scales.astype(np.float64) - 127.0), 8, axis=1)[..., None]
    return vals.transpose(0, 1, 3, 2).reshape(g * 512, n)


D, T, I, Q, E, G = 512, 2048, 1024, 128, 512, 64


def setup_inputs():
    n = np.random.standard_normal
    idx = (np.random.permutation(T // 16)[:I // 16, None] * 16 + np.arange(16)).reshape(-1)
    fd = mx_kscale(D)
    fi = mx_kscale(I)
    ti = np.ones(T)
    ti[idx] = fi
    keysp = pack_weight(n((D, T)) / fd[:, None], "e4m3")
    return {
        "query": (n((D, Q)) * 0.25 / np.sqrt(D) * fd[:, None]).astype(np.float32),
        "keys_words": keysp[0],
        "keys_scales": keysp[1],
        "size": (np.random.uniform(0.5, 2.0, (1, I)) * fi).astype(np.float32),
        "vals": (n((E, T)) / ti).astype(np.float32),
        "offs": striped(idx),
    }


def reference(query, keys_words, keys_scales, size, vals, offs):
    idx = unstriped(offs)
    keysu = unpack_weight(keys_words, keys_scales, "e4m3")
    queryq = mxq(f64(query), 0, "e4m3")
    keysidxg = keysu[:, idx]
    a = queryq.T @ keysidxg
    m = a.reshape(Q, G, I // G).max(axis=2)
    r = np.exp(m - np.max(m, axis=1, keepdims=True))
    p = np.exp(a)
    z = p.reshape(Q, G, I // G).sum(axis=2)
    f = r / np.sum(r, axis=1, keepdims=True) / z
    fr = np.repeat(f, I // G, axis=1)
    w = p * fr * f64(size)
    wt = w.T
    vt = f64(vals)[:, idx].T
    wtq = mxq(wt, 0, "e4m3")
    vtq = mxq(vt, 0, "e4m3")
    o = wtq.T @ vtq
    return o

@@ -1,0 +1,213 @@
+from contextlib import ExitStack
+
+import concourse.mybir as mybir
+
+D, T, I, Q, E, G = 512, 2048, 1024, 128, 512, 64
+FLOPS = 2 * Q * I * D + 2 * Q * I * E
+
+F32 = mybir.dt.float32
+BF16 = mybir.dt.bfloat16
+I32 = mybir.dt.int32
+U32 = mybir.dt.uint32
+U16 = mybir.dt.uint16
+U8 = mybir.dt.uint8
+FP8X4 = mybir.dt.float8_e4m3fn_x4
+ACT = mybir.ActivationFunctionType
+ALU = mybir.AluOpType
+AX = mybir.AxisListType
+
+P = 128
+PACK = 4
+SLOTS = P * PACK
+PASSES = I // SLOTS
+PLANES = E // P
+LIST_COLS = SLOTS // 16
+TINY = 1e-30
+SCALAR_PLANES = 2
+PLANE_BYTES = 4 * T
+SPARE = 4 * PLANE_BYTES + 4 * SLOTS + 64 + I
+SPARE_BYTES = 2 * I + 2 * G
+
+
+def tile_attend_docmix_kernel(tc, query, keys_words, keys_scales, size, vals, offs, out):
+    nc = tc.nc
+    with ExitStack() as ctx:
+        keep = ctx.enter_context(tc.tile_pool(name="keep", bufs=1))
+        early = ctx.enter_context(tc.tile_pool(name="early", bufs=1))
+        psum = ctx.enter_context(tc.psum_pool(name="psum", bufs=1))
+        turn = ctx.enter_context(tc.psum_pool(name="turn", bufs=3))
+
+        offsets = keep.tile([P, I // 16], U16, name="offsets")
+        nc.sync.dma_start(offsets[:], offs)
+        first_plane = early.tile([P, T], F32, name="first_plane", align_bytes=64, offset=0)
+        nc.sync.dma_start(first_plane[:], vals[0:P, :])
+
+        scale_pool = keep.tile([P, T], U8, name="scale_pool", align_bytes=64)
+        nc.vector.memset(scale_pool[:].bitcast(I32), 0)
+        for r in range(4):
+            nc.sync.dma_start(scale_pool[r:P:32, :].bitcast(I32), keys_scales[0, r:16:4, :].bitcast(I32))
+
+        warm = keep.tile([P, 1], F32, name="warm")
+        nc.vector.memset(warm[:], 0.0)
+        warmed = keep.tile([P, 1], F32, name="warmed")
+        nc.scalar.activation(warmed[:], warm[:], ACT.Exp)
+
+        ident = keep.tile([P, P], F32, name="ident")
+        with tc.tile_pool(name="setup", bufs=1) as setup:
+            zeros = setup.tile([P, PLANES * T + SLOTS + 16], F32, name="zeros", align_bytes=64)
+            nc.gpsimd.memset(zeros[:, :P], 0.0)
+            nc.gpsimd.affine_select(
+                out=ident[:], in_=zeros[:, :P], compare_op=ALU.not_equal, fill=1.0,
+                base=0, pattern=[[-1, P]], channel_multiplier=1,
+            )
+        pools = ctx.enter_context(tc.tile_pool(name="pools", bufs=1))
+        q_raw = pools.tile([P, PACK, Q], F32, name="q_raw", align_bytes=64, offset=4 * PLANE_BYTES)
+        nc.sync.dma_start(q_raw[:], query.rearrange("(p t) q -> p t q", t=PACK))
+        word_pool = pools.tile([P, T], I32, name="word_pool", align_bytes=64, offset=3 * PLANE_BYTES)
+        nc.sync.dma_start(word_pool[:], keys_words[0].rearrange("p c r -> p (c r)").bitcast(I32))
+        val_pool = [first_plane]
+        size_cols = pools.tile([P, PASSES, PACK], F32, name="size_cols", align_bytes=64, offset=4 * PLANE_BYTES + 4 * SLOTS)
+        for c in range(1, PLANES):
+            plane = pools.tile([P, T], F32, name="val_pool%d" % c, align_bytes=64, offset=(c - 1) * PLANE_BYTES)
+            nc.sync.dma_start(plane[:], vals[c * P : (c + 1) * P, :])
+            val_pool.append(plane)
+            if c == 1:
+                nc.sync.dma_start(size_cols[:], size[0].rearrange("(h s t) -> s h t", h=PASSES, t=PACK))
+
+        def listed(window, h):
+            return window.indirect(offsets[:, h * LIST_COLS : (h + 1) * LIST_COLS])
+
+        v_codes = keep.tile([P, PASSES * E], U32, name="v_codes", align_bytes=64)
+
+        def cast_plane(c):
+            cast = early.tile([P, T], BF16, name="val_cast%d" % c, align_bytes=64, offset=PLANE_BYTES)
+            nc.scalar.activation(cast[:], val_pool[c][:], ACT.Copy)
+            return cast
+
+        def value_unit(c, h, window, picked):
+            if c < SCALAR_PLANES:
+                nc.scalar.activation(picked[:], listed(window[:], h), ACT.Copy)
+            else:
+                nc.vector.tensor_copy(picked[:], listed(window[:], h))
+            pairs = picked[:].bitcast(F32)
+            turned = turn.tile([P, 2, P], F32, name="turned")
+            for u in range(2):
+                nc.tensor.transpose(turned[:, u, :], pairs[:, u : SLOTS // 2 : 2], ident[:])
+            v_bf = keep.tile([P, P, PACK], BF16, name="v_bf%d_%d" % (c, h), align_bytes=64)
+            nc.scalar.copy(v_bf[:].bitcast(F32), turned[:].rearrange("s u e -> s e u"))
+            cols = slice(h * E + c * P, h * E + (c + 1) * P)
+            nc.vector.quantize_mx(v_codes[:, cols].bitcast(FP8X4), v_scales[:, cols], v_bf[:].rearrange("s e t -> s (e t)"))
+
+        cast0 = cast_plane(0)
+
+        key_scales = keep.tile([P, I], U8, name="key_scales", align_bytes=64)
+        nc.vector.tensor_copy(key_scales[:], scale_pool[:].indirect(offsets[:]))
+
+        q_bf = early.tile([P, Q, PACK], BF16, name="q_bf", align_bytes=64, offset=0)
+        nc.scalar.copy(q_bf[:], q_raw[:].rearrange("p t q -> p q t"))
+        q_codes = keep.tile([P, Q], U32, name="q_codes", align_bytes=64)
+        q_scales = keep.tile([P, Q], U8, name="q_scales", align_bytes=64)
+        nc.vector.quantize_mx(q_codes[:].bitcast(FP8X4), q_scales[:], q_bf[:].rearrange("p q t -> p (q t)"))
+
+        scores = []
+        for h in range(PASSES):
+            key_words = keep.tile([P, SLOTS], U32, name="key_words%d" % h, align_bytes=64)
+            nc.vector.tensor_copy(key_words[:], listed(word_pool[:].bitcast(U32), h))
+            score = psum.tile([P, SLOTS], F32, name="score%d" % h)
+            nc.tensor.matmul_mx(
+                score[:], q_codes[:].bitcast(FP8X4), q_scales[:],
+                key_words[:].bitcast(FP8X4), key_scales[:, h * SLOTS : (h + 1) * SLOTS],
+                start=True, stop=True,
+            )
+            scores.append(score)
+
+        best = pools.tile([P, G], F32, name="best", align_bytes=64, offset=SPARE)
+        for h in range(PASSES):
+            nc.vector.tensor_reduce(
+                best[:, h * (G // PASSES) : (h + 1) * (G // PASSES)],
+                scores[h][:].rearrange("q (g j) -> q g j", j=16), AX.X, ALU.max,
+            )
+        v_scales = pools.tile([P, PASSES * E], U8, name="v_scales", align_bytes=64, offset=SPARE + 2 * G - I)
+        neg_top = pools.tile([P, 1], F32, name="neg_top", align_bytes=64, offset=SPARE + SPARE_BYTES)
+        nc.vector.tensor_reduce(neg_top[:], best[:], AX.X, ALU.max, negate=True)
+
+        picked0 = pools.tile([P, PASSES, SLOTS], BF16, name="picked0", align_bytes=64, offset=4 * PLANE_BYTES)
+        for h in range(PASSES):
+            value_unit(0, h, cast0, picked0[:, h, :])
+        cast1 = cast_plane(1)
+
+        share = pools.tile([P, G], F32, name="share", align_bytes=64, offset=0)
+        share_sum = keep.tile([P, 1], F32, name="share_sum")
+        nc.scalar.activation(share[:], best[:], ACT.Exp, bias=neg_top[:], accum_out=share_sum[:])
+        prob = pools.tile([P, PACK, PASSES, P], F32, name="prob", align_bytes=64, offset=PLANE_BYTES // 2)
+        for h in range(PASSES):
+            nc.scalar.activation(
+                prob[:, :, h, :], scores[h][:].rearrange("q (s t) -> q t s", t=PACK), ACT.Exp, bias=neg_top[:],
+            )
+
+        picked2 = pools.tile([P, PASSES, SLOTS], BF16, name="picked2", align_bytes=64, offset=SPARE + 2 * G)
+        for h in range(PASSES):
+            value_unit(2, h, val_pool[2], picked2[:, h, :])
+
+        z = pools.tile([P, G], F32, name="z", align_bytes=64, offset=PLANE_BYTES)
+        nc.vector.tensor_reduce(z[:], prob[:].rearrange("q t h (g j) -> q (h g) t j", j=PACK), AX.XY, ALU.add)
+        denom = keep.tile([P, G], F32, name="denom")
+        nc.vector.tensor_scalar(denom[:], z[:], TINY, share_sum[:], ALU.max, ALU.mult)
+        inv = pools.tile([P, G], F32, name="inv", align_bytes=64, offset=SPARE + 2 * SPARE_BYTES)
+        nc.vector.reciprocal(inv[:], denom[:])
+        factor = keep.tile([P, G, PACK], F32, name="factor")
+        nc.vector.tensor_tensor(
+            factor[:], share[:].unsqueeze(2).to_broadcast([P, G, PACK]), inv[:].unsqueeze(2).to_broadcast([P, G, PACK]), ALU.mult,
+        )
+
+        sized = []
+        for h in range(PASSES):
+            prob_t = psum.tile([P, PACK, Q], F32, name="prob_t%d" % h)
+            for t in range(PACK):
+                nc.tensor.transpose(prob_t[:, t, :], prob[:, t, h, :], ident[:])
+            sized_h = keep.tile([P, PACK, Q], F32, name="sized%d" % h)
+            for t in range(PACK):
+                nc.scalar.activation(sized_h[:, t, :], prob_t[:, t, :], ACT.Copy, scale=size_cols[:, h, t : t + 1])
+            sized.append(sized_h)
+
+        factor_t = psum.tile([P, PASSES, Q], F32, name="factor_t")
+        factor_cols = factor[:].rearrange("q (h g) j -> q h (g j)", h=PASSES)
+        for h in range(PASSES):
+            nc.tensor.transpose(factor_t[:, h, :], factor_cols[:, h, :], ident[:])
+
+        picked1 = pools.tile([P, PASSES, SLOTS], BF16, name="picked1", align_bytes=64, offset=SPARE + SPARE_BYTES)
+        for h in range(PASSES):
+            value_unit(1, h, cast1, picked1[:, h, :])
+        value_unit(3, 0, val_pool[3], pools.tile([P, SLOTS], BF16, name="picked3_0", align_bytes=64, offset=PLANE_BYTES // 2))
+        value_unit(3, 1, val_pool[3], pools.tile([P, SLOTS], BF16, name="picked3_1", align_bytes=64, offset=SPARE + 2 * SPARE_BYTES))
+
+        w_codes = keep.tile([P, PASSES * Q], U32, name="w_codes", align_bytes=64)
+        w_scales = keep.tile([P, PASSES * Q], U8, name="w_scales", align_bytes=64)
+        for h in range(PASSES):
+            w_bf = keep.tile([P, Q, PACK], BF16, name="w_bf%d" % h, align_bytes=64)
+            nc.vector.tensor_tensor(
+                w_bf[:].rearrange("s (c i) t -> s c t i", i=4),
+                sized[h][:].rearrange("s t (c i) -> s c t i", i=4),
+                factor_t[:, h, :].rearrange("s (c i) -> s c i", i=4).unsqueeze(2).to_broadcast([P, Q // 4, PACK, 4]),
+                ALU.mult,
+            )
+            nc.vector.quantize_mx(
+                w_codes[:, h * Q : (h + 1) * Q].bitcast(FP8X4), w_scales[:, h * Q : (h + 1) * Q],
+                w_bf[:].rearrange("s q t -> s (q t)"),
+            )
+
+        half = E // 2
+        accs = [psum.tile([P, half], F32, name="score%d" % b) for b in range(2)]
+        for h in range(PASSES):
+            for b in range(2):
+                cols = slice(h * E + b * half, h * E + (b + 1) * half)
+                nc.tensor.matmul_mx(
+                    accs[b][:], w_codes[:, h * Q : (h + 1) * Q].bitcast(FP8X4), w_scales[:, h * Q : (h + 1) * Q],
+                    v_codes[:, cols].bitcast(FP8X4), v_scales[:, cols],
+                    start=(h == 0), stop=(h == PASSES - 1),
+                )
+        results = [keep.tile([P, half], F32, name="result%d" % b) for b in range(2)]
+        nc.scalar.copy(results[0][:], accs[0][:])
+        nc.vector.tensor_copy(results[1][:], accs[1][:])
+        nc.scalar.dma_start(out[:, :half], results[0][:])
+        nc.sync.dma_start(out[:, half:], results[1][:])

@@ -23,24 +23,25 @@ PASSES = I // SLOTS
 PLANES = E // P
 LIST_COLS = SLOTS // 16
 TINY = 1e-30
-SCALAR_PLANES = 2
 PLANE_BYTES = 4 * T
-SPARE = 4 * PLANE_BYTES + 4 * SLOTS + 64 + I
-SPARE_BYTES = 2 * I + 2 * G
+HALF = T // 2
+AT_THIRD, AT_LOADS, AT_CAST = 0, PLANE_BYTES, 5 * PLANE_BYTES
+AT_WORDS = AT_CAST + PLANE_BYTES
+AT_BEST = AT_WORDS + PLANE_BYTES
+AT_CAST1 = AT_BEST + 2 * G
 
 
 def tile_attend_docmix_kernel(tc, query, keys_words, keys_scales, size, vals, offs, out):
     nc = tc.nc
     with ExitStack() as ctx:
         keep = ctx.enter_context(tc.tile_pool(name="keep", bufs=1))
-        early = ctx.enter_context(tc.tile_pool(name="early", bufs=1))
         psum = ctx.enter_context(tc.psum_pool(name="psum", bufs=1))
         turn = ctx.enter_context(tc.psum_pool(name="turn", bufs=3))
 
         offsets = keep.tile([P, I // 16], U16, name="offsets")
         nc.sync.dma_start(offsets[:], offs)
-        first_plane = early.tile([P, T], F32, name="first_plane", align_bytes=64, offset=0)
-        nc.sync.dma_start(first_plane[:], vals[0:P, :])
+        left = keep.tile([P, HALF], F32, name="left", align_bytes=64)
+        nc.sync.dma_start(left[:], vals[0:P, :HALF])
 
         scale_pool = keep.tile([P, T], U8, name="scale_pool", align_bytes=64)
         nc.vector.memset(scale_pool[:].bitcast(I32), 0)
@@ -54,65 +55,68 @@ def tile_attend_docmix_kernel(tc, query, keys_words, keys_scales, size, vals, of
 
         ident = keep.tile([P, P], F32, name="ident")
         with tc.tile_pool(name="setup", bufs=1) as setup:
-            zeros = setup.tile([P, PLANES * T + SLOTS + 16], F32, name="zeros", align_bytes=64)
+            zeros = setup.tile([P, AT_CAST // 4], F32, name="zeros", align_bytes=64)
             nc.gpsimd.memset(zeros[:, :P], 0.0)
             nc.gpsimd.affine_select(
                 out=ident[:], in_=zeros[:, :P], compare_op=ALU.not_equal, fill=1.0,
                 base=0, pattern=[[-1, P]], channel_multiplier=1,
             )
-        pools = ctx.enter_context(tc.tile_pool(name="pools", bufs=1))
-        q_raw = pools.tile([P, PACK, Q], F32, name="q_raw", align_bytes=64, offset=4 * PLANE_BYTES)
-        nc.sync.dma_start(q_raw[:], query.rearrange("(p t) q -> p t q", t=PACK))
-        word_pool = pools.tile([P, T], I32, name="word_pool", align_bytes=64, offset=3 * PLANE_BYTES)
-        nc.sync.dma_start(word_pool[:], keys_words[0].rearrange("p c r -> p (c r)").bitcast(I32))
-        val_pool = [first_plane]
-        size_cols = pools.tile([P, PASSES, PACK], F32, name="size_cols", align_bytes=64, offset=4 * PLANE_BYTES + 4 * SLOTS)
-        for c in range(1, PLANES):
-            plane = pools.tile([P, T], F32, name="val_pool%d" % c, align_bytes=64, offset=(c - 1) * PLANE_BYTES)
-            nc.sync.dma_start(plane[:], vals[c * P : (c + 1) * P, :])
-            val_pool.append(plane)
-            if c == 1:
-                nc.sync.dma_start(size_cols[:], size[0].rearrange("(h s t) -> s h t", h=PASSES, t=PACK))
+        arena = ctx.enter_context(tc.tile_pool(name="arena", bufs=1))
 
-        def listed(window, h):
-            return window.indirect(offsets[:, h * LIST_COLS : (h + 1) * LIST_COLS])
+        def placed(name, shape, dtype, at):
+            return arena.tile(shape, dtype, name=name, align_bytes=64, offset=at)
+
+        q_raw = placed("q_raw", [P, PACK, Q], F32, AT_LOADS)
+        nc.sync.dma_start(q_raw[:], query.rearrange("(p t) q -> p t q", t=PACK))
+        word_pool = placed("word_pool", [P, T], I32, AT_LOADS + PLANE_BYTES)
+        nc.sync.dma_start(word_pool[:], keys_words[0].rearrange("p c r -> p (c r)").bitcast(I32))
+        right = placed("right", [P, HALF], F32, AT_LOADS + PLANE_BYTES // 2)
+        nc.sync.dma_start(right[:], vals[0:P, HALF:])
+        plane2 = placed("plane2", [P, T], F32, AT_THIRD)
+        nc.sync.dma_start(plane2[:], vals[2 * P : 3 * P, :])
+        size_cols = placed("size_cols", [P, PASSES, PACK], F32, AT_LOADS + PLANE_BYTES // 4)
+        nc.sync.dma_start(size_cols[:], size[0].rearrange("(h s t) -> s h t", h=PASSES, t=PACK))
+        plane1 = placed("plane1", [P, T], F32, AT_LOADS + 2 * PLANE_BYTES)
+        nc.sync.dma_start(plane1[:], vals[P : 2 * P, :])
+        plane3 = placed("plane3", [P, T], F32, AT_LOADS + 3 * PLANE_BYTES)
+        nc.sync.dma_start(plane3[:], vals[3 * P : 4 * P, :])
+
+        def listed(window, first, count):
+            return window.indirect(offsets[:, first // 16 : (first + count) // 16])
 
         v_codes = keep.tile([P, PASSES * E], U32, name="v_codes", align_bytes=64)
 
-        def cast_plane(c):
-            cast = early.tile([P, T], BF16, name="val_cast%d" % c, align_bytes=64, offset=PLANE_BYTES)
-            nc.scalar.activation(cast[:], val_pool[c][:], ACT.Copy)
-            return cast
+        def turn_and_quantise(c, passes, picked, v_bf):
+            turned = turn.tile([P, len(passes), 2, P], F32, name="turned")
+            for n, h in enumerate(passes):
+                pairs = picked[:, h * SLOTS : (h + 1) * SLOTS].bitcast(F32)
+                for u in range(2):
+                    nc.tensor.transpose(turned[:, n, u, :], pairs[:, u : SLOTS // 2 : 2], ident[:])
+            nc.scalar.copy(v_bf[:].bitcast(F32), turned[:].rearrange("s h u e -> s h e u"))
+            cols = slice((c * PASSES + passes[0]) * P, (c * PASSES + passes[-1] + 1) * P)
+            nc.vector.quantize_mx(
+                v_codes[:, cols].bitcast(FP8X4), v_scales[:, cols], v_bf[:].rearrange("s h e t -> s (h e t)"),
+            )
 
-        def value_unit(c, h, window, picked):
-            if c < SCALAR_PLANES:
-                nc.scalar.activation(picked[:], listed(window[:], h), ACT.Copy)
-            else:
-                nc.vector.tensor_copy(picked[:], listed(window[:], h))
-            pairs = picked[:].bitcast(F32)
-            turned = turn.tile([P, 2, P], F32, name="turned")
-            for u in range(2):
-                nc.tensor.transpose(turned[:, u, :], pairs[:, u : SLOTS // 2 : 2], ident[:])
-            v_bf = keep.tile([P, P, PACK], BF16, name="v_bf%d_%d" % (c, h), align_bytes=64)
-            nc.scalar.copy(v_bf[:].bitcast(F32), turned[:].rearrange("s u e -> s e u"))
-            cols = slice(h * E + c * P, h * E + (c + 1) * P)
-            nc.vector.quantize_mx(v_codes[:, cols].bitcast(FP8X4), v_scales[:, cols], v_bf[:].rearrange("s e t -> s (e t)"))
-
-        cast0 = cast_plane(0)
+        cast0 = placed("cast0", [P, T], BF16, AT_CAST)
+        nc.scalar.activation(cast0[:, :HALF], left[:], ACT.Copy)
+        nc.scalar.activation(cast0[:, HALF:], right[:], ACT.Copy)
 
         key_scales = keep.tile([P, I], U8, name="key_scales", align_bytes=64)
         nc.vector.tensor_copy(key_scales[:], scale_pool[:].indirect(offsets[:]))
 
-        q_bf = early.tile([P, Q, PACK], BF16, name="q_bf", align_bytes=64, offset=0)
-        nc.scalar.copy(q_bf[:], q_raw[:].rearrange("p t q -> p q t"))
+        q_bf = keep.tile([P, Q, PACK], BF16, name="q_bf", align_bytes=64)
+        nc.vector.tensor_copy(
+            q_bf[:].rearrange("p (c i) t -> p c t i", i=4), q_raw[:].rearrange("p t (c i) -> p c t i", i=4),
+        )
         q_codes = keep.tile([P, Q], U32, name="q_codes", align_bytes=64)
         q_scales = keep.tile([P, Q], U8, name="q_scales", align_bytes=64)
         nc.vector.quantize_mx(q_codes[:].bitcast(FP8X4), q_scales[:], q_bf[:].rearrange("p q t -> p (q t)"))
 
         scores = []
         for h in range(PASSES):
-            key_words = keep.tile([P, SLOTS], U32, name="key_words%d" % h, align_bytes=64)
-            nc.vector.tensor_copy(key_words[:], listed(word_pool[:].bitcast(U32), h))
+            key_words = placed("key_words%d" % h, [P, SLOTS], U32, AT_WORDS + h * 4 * SLOTS)
+            nc.vector.tensor_copy(key_words[:], listed(word_pool[:].bitcast(U32), h * SLOTS, SLOTS))
             score = psum.tile([P, SLOTS], F32, name="score%d" % h)
             nc.tensor.matmul_mx(
                 score[:], q_codes[:].bitcast(FP8X4), q_scales[:],
@@ -121,39 +125,44 @@ def tile_attend_docmix_kernel(tc, query, keys_words, keys_scales, size, vals, of
             )
             scores.append(score)
 
-        best = pools.tile([P, G], F32, name="best", align_bytes=64, offset=SPARE)
+        best = placed("best", [P, G], F32, AT_BEST)
         for h in range(PASSES):
             nc.vector.tensor_reduce(
                 best[:, h * (G // PASSES) : (h + 1) * (G // PASSES)],
                 scores[h][:].rearrange("q (g j) -> q g j", j=16), AX.X, ALU.max,
             )
-        v_scales = pools.tile([P, PASSES * E], U8, name="v_scales", align_bytes=64, offset=SPARE + 2 * G - I)
-        neg_top = pools.tile([P, 1], F32, name="neg_top", align_bytes=64, offset=SPARE + SPARE_BYTES)
+        neg_top = keep.tile([P, 1], F32, name="neg_top")
         nc.vector.tensor_reduce(neg_top[:], best[:], AX.X, ALU.max, negate=True)
 
-        picked0 = pools.tile([P, PASSES, SLOTS], BF16, name="picked0", align_bytes=64, offset=4 * PLANE_BYTES)
+        picked0 = placed("picked0", [P, I], BF16, AT_WORDS)
         for h in range(PASSES):
-            value_unit(0, h, cast0, picked0[:, h, :])
-        cast1 = cast_plane(1)
+            nc.scalar.activation(picked0[:, h * SLOTS : (h + 1) * SLOTS], listed(cast0[:], h * SLOTS, SLOTS), ACT.Copy)
 
-        share = pools.tile([P, G], F32, name="share", align_bytes=64, offset=0)
+        share = placed("share", [P, G], F32, AT_CAST)
         share_sum = keep.tile([P, 1], F32, name="share_sum")
         nc.scalar.activation(share[:], best[:], ACT.Exp, bias=neg_top[:], accum_out=share_sum[:])
-        prob = pools.tile([P, PACK, PASSES, P], F32, name="prob", align_bytes=64, offset=PLANE_BYTES // 2)
+        prob = placed("prob", [P, PACK, PASSES, P], F32, AT_CAST + 4 * G)
         for h in range(PASSES):
             nc.scalar.activation(
                 prob[:, :, h, :], scores[h][:].rearrange("q (s t) -> q t s", t=PACK), ACT.Exp, bias=neg_top[:],
             )
 
-        picked2 = pools.tile([P, PASSES, SLOTS], BF16, name="picked2", align_bytes=64, offset=SPARE + 2 * G)
-        for h in range(PASSES):
-            value_unit(2, h, val_pool[2], picked2[:, h, :])
+        v_scales = placed("v_scales", [P, PASSES * E], U8, AT_CAST + 4 * G + 2 * I)
+        turn_and_quantise(0, (0, 1), picked0, keep.tile([P, PASSES, P, PACK], BF16, name="v_bf0", align_bytes=64))
 
-        z = pools.tile([P, G], F32, name="z", align_bytes=64, offset=PLANE_BYTES)
+        picked2 = placed("picked2", [P, I], BF16, AT_WORDS + 4 * SLOTS)
+        for h in range(PASSES):
+            nc.vector.tensor_copy(picked2[:, h * SLOTS : (h + 1) * SLOTS], listed(plane2[:], h * SLOTS, SLOTS))
+
+        cast1 = placed("cast1", [P, T], BF16, AT_CAST1)
+        nc.vector.tensor_copy(cast1[:, :HALF], plane1[:, :HALF])
+        nc.scalar.activation(cast1[:, HALF:], plane1[:, HALF:], ACT.Copy)
+
+        z = placed("z", [P, G], F32, AT_THIRD)
         nc.vector.tensor_reduce(z[:], prob[:].rearrange("q t h (g j) -> q (h g) t j", j=PACK), AX.XY, ALU.add)
         denom = keep.tile([P, G], F32, name="denom")
         nc.vector.tensor_scalar(denom[:], z[:], TINY, share_sum[:], ALU.max, ALU.mult)
-        inv = pools.tile([P, G], F32, name="inv", align_bytes=64, offset=SPARE + 2 * SPARE_BYTES)
+        inv = keep.tile([P, G], F32, name="inv")
         nc.vector.reciprocal(inv[:], denom[:])
         factor = keep.tile([P, G, PACK], F32, name="factor")
         nc.vector.tensor_tensor(
@@ -175,16 +184,16 @@ def tile_attend_docmix_kernel(tc, query, keys_words, keys_scales, size, vals, of
         for h in range(PASSES):
             nc.tensor.transpose(factor_t[:, h, :], factor_cols[:, h, :], ident[:])
 
-        picked1 = pools.tile([P, PASSES, SLOTS], BF16, name="picked1", align_bytes=64, offset=SPARE + SPARE_BYTES)
+        turn_and_quantise(2, (0, 1), picked2, keep.tile([P, PASSES, P, PACK], BF16, name="v_bf2", align_bytes=64))
+
+        picked3 = placed("picked3", [P, I], BF16, AT_CAST + 4 * G)
         for h in range(PASSES):
-            value_unit(1, h, cast1, picked1[:, h, :])
-        value_unit(3, 0, val_pool[3], pools.tile([P, SLOTS], BF16, name="picked3_0", align_bytes=64, offset=PLANE_BYTES // 2))
-        value_unit(3, 1, val_pool[3], pools.tile([P, SLOTS], BF16, name="picked3_1", align_bytes=64, offset=SPARE + 2 * SPARE_BYTES))
+            nc.vector.tensor_copy(picked3[:, h * SLOTS : (h + 1) * SLOTS], listed(plane3[:], h * SLOTS, SLOTS))
 
         w_codes = keep.tile([P, PASSES * Q], U32, name="w_codes", align_bytes=64)
         w_scales = keep.tile([P, PASSES * Q], U8, name="w_scales", align_bytes=64)
         for h in range(PASSES):
-            w_bf = keep.tile([P, Q, PACK], BF16, name="w_bf%d" % h, align_bytes=64)
+            w_bf = placed("w_bf%d" % h, [P, Q, PACK], BF16, AT_LOADS + 3 * PLANE_BYTES + h * 2 * SLOTS)
             nc.vector.tensor_tensor(
                 w_bf[:].rearrange("s (c i) t -> s c t i", i=4),
                 sized[h][:].rearrange("s t (c i) -> s c t i", i=4),
@@ -196,18 +205,27 @@ def tile_attend_docmix_kernel(tc, query, keys_words, keys_scales, size, vals, of
                 w_bf[:].rearrange("s q t -> s (q t)"),
             )
 
-        half = E // 2
-        accs = [psum.tile([P, half], F32, name="score%d" % b) for b in range(2)]
+        picked1 = keep.tile([P, I], BF16, name="picked1", align_bytes=64)
         for h in range(PASSES):
-            for b in range(2):
-                cols = slice(h * E + b * half, h * E + (b + 1) * half)
-                nc.tensor.matmul_mx(
-                    accs[b][:], w_codes[:, h * Q : (h + 1) * Q].bitcast(FP8X4), w_scales[:, h * Q : (h + 1) * Q],
-                    v_codes[:, cols].bitcast(FP8X4), v_scales[:, cols],
-                    start=(h == 0), stop=(h == PASSES - 1),
-                )
-        results = [keep.tile([P, half], F32, name="result%d" % b) for b in range(2)]
-        nc.scalar.copy(results[0][:], accs[0][:])
-        nc.vector.tensor_copy(results[1][:], accs[1][:])
-        nc.scalar.dma_start(out[:, :half], results[0][:])
-        nc.sync.dma_start(out[:, half:], results[1][:])
+            nc.scalar.activation(picked1[:, h * SLOTS : (h + 1) * SLOTS], listed(cast1[:], h * SLOTS, SLOTS), ACT.Copy)
+            turn_and_quantise(1, (h,), picked1, keep.tile([P, 1, P, PACK], BF16, name="v_bf1_%d" % h, align_bytes=64))
+
+        turn_and_quantise(3, (0, 1), picked3, placed("v_bf3", [P, PASSES, P, PACK], BF16, AT_CAST1))
+
+        for b in range(2):
+            acc = psum.tile([P, 2, P], F32, name="score%d" % b)
+            for n in range(2):
+                for h in range(PASSES):
+                    cols = slice(((2 * b + n) * PASSES + h) * P, ((2 * b + n) * PASSES + h + 1) * P)
+                    nc.tensor.matmul_mx(
+                        acc[:, n, :], w_codes[:, h * Q : (h + 1) * Q].bitcast(FP8X4), w_scales[:, h * Q : (h + 1) * Q],
+                        v_codes[:, cols].bitcast(FP8X4), v_scales[:, cols],
+                        start=(h == 0), stop=(h == PASSES - 1),
+                    )
+            result = keep.tile([P, 2 * P], F32, name="result%d" % b)
+            if b == 0:
+                nc.scalar.copy(result[:], acc[:].rearrange("q n e -> q (n e)"))
+                nc.scalar.dma_start(out[:, : 2 * P], result[:])
+            else:
+                nc.vector.tensor_copy(result[:], acc[:].rearrange("q n e -> q (n e)"))
+                nc.sync.dma_start(out[:, 2 * P :], result[:])

from contextlib import ExitStack

import concourse.mybir as mybir

D, T, I, Q, E, G = 512, 2048, 1024, 128, 512, 64
FLOPS = 2 * Q * I * D + 2 * Q * I * E

F32 = mybir.dt.float32
BF16 = mybir.dt.bfloat16
I32 = mybir.dt.int32
U32 = mybir.dt.uint32
U16 = mybir.dt.uint16
U8 = mybir.dt.uint8
FP8X4 = mybir.dt.float8_e4m3fn_x4
ACT = mybir.ActivationFunctionType
ALU = mybir.AluOpType
AX = mybir.AxisListType

P = 128
PACK = 4
SLOTS = P * PACK
PASSES = I // SLOTS
PLANES = E // P
LIST_COLS = SLOTS // 16
TINY = 1e-30
PLANE_BYTES = 4 * T
HALF = T // 2
AT_THIRD, AT_LOADS, AT_CAST = 0, PLANE_BYTES, 5 * PLANE_BYTES
AT_WORDS = AT_CAST + PLANE_BYTES
AT_BEST = AT_WORDS + PLANE_BYTES
AT_CAST1 = AT_BEST + 2 * G


def tile_attend_docmix_kernel(tc, query, keys_words, keys_scales, size, vals, offs, out):
    nc = tc.nc
    with ExitStack() as ctx:
        keep = ctx.enter_context(tc.tile_pool(name="keep", bufs=1))
        psum = ctx.enter_context(tc.psum_pool(name="psum", bufs=1))
        turn = ctx.enter_context(tc.psum_pool(name="turn", bufs=3))

        offsets = keep.tile([P, I // 16], U16, name="offsets")
        nc.sync.dma_start(offsets[:], offs)
        left = keep.tile([P, HALF], F32, name="left", align_bytes=64)
        nc.sync.dma_start(left[:], vals[0:P, :HALF])

        scale_pool = keep.tile([P, T], U8, name="scale_pool", align_bytes=64)
        nc.vector.memset(scale_pool[:].bitcast(I32), 0)
        for r in range(4):
            nc.sync.dma_start(scale_pool[r:P:32, :].bitcast(I32), keys_scales[0, r:16:4, :].bitcast(I32))

        warm = keep.tile([P, 1], F32, name="warm")
        nc.vector.memset(warm[:], 0.0)
        warmed = keep.tile([P, 1], F32, name="warmed")
        nc.scalar.activation(warmed[:], warm[:], ACT.Exp)

        ident = keep.tile([P, P], F32, name="ident")
        with tc.tile_pool(name="setup", bufs=1) as setup:
            zeros = setup.tile([P, AT_CAST // 4], F32, name="zeros", align_bytes=64)
            nc.gpsimd.memset(zeros[:, :P], 0.0)
            nc.gpsimd.affine_select(
                out=ident[:], in_=zeros[:, :P], compare_op=ALU.not_equal, fill=1.0,
                base=0, pattern=[[-1, P]], channel_multiplier=1,
            )
        arena = ctx.enter_context(tc.tile_pool(name="arena", bufs=1))

        def placed(name, shape, dtype, at):
            return arena.tile(shape, dtype, name=name, align_bytes=64, offset=at)

        q_raw = placed("q_raw", [P, PACK, Q], F32, AT_LOADS)
        nc.sync.dma_start(q_raw[:], query.rearrange("(p t) q -> p t q", t=PACK))
        word_pool = placed("word_pool", [P, T], I32, AT_LOADS + PLANE_BYTES)
        nc.sync.dma_start(word_pool[:], keys_words[0].rearrange("p c r -> p (c r)").bitcast(I32))
        right = placed("right", [P, HALF], F32, AT_LOADS + PLANE_BYTES // 2)
        nc.sync.dma_start(right[:], vals[0:P, HALF:])
        plane2 = placed("plane2", [P, T], F32, AT_THIRD)
        nc.sync.dma_start(plane2[:], vals[2 * P : 3 * P, :])
        size_cols = placed("size_cols", [P, PASSES, PACK], F32, AT_LOADS + PLANE_BYTES // 4)
        nc.sync.dma_start(size_cols[:], size[0].rearrange("(h s t) -> s h t", h=PASSES, t=PACK))
        plane1 = placed("plane1", [P, T], F32, AT_LOADS + 2 * PLANE_BYTES)
        nc.sync.dma_start(plane1[:], vals[P : 2 * P, :])
        plane3 = placed("plane3", [P, T], F32, AT_LOADS + 3 * PLANE_BYTES)
        nc.sync.dma_start(plane3[:], vals[3 * P : 4 * P, :])

        def listed(window, first, count):
            return window.indirect(offsets[:, first // 16 : (first + count) // 16])

        v_codes = keep.tile([P, PASSES * E], U32, name="v_codes", align_bytes=64)

        def turn_and_quantise(c, passes, picked, v_bf):
            turned = turn.tile([P, len(passes), 2, P], F32, name="turned")
            for n, h in enumerate(passes):
                pairs = picked[:, h * SLOTS : (h + 1) * SLOTS].bitcast(F32)
                for u in range(2):
                    nc.tensor.transpose(turned[:, n, u, :], pairs[:, u : SLOTS // 2 : 2], ident[:])
            nc.scalar.copy(v_bf[:].bitcast(F32), turned[:].rearrange("s h u e -> s h e u"))
            cols = slice((c * PASSES + passes[0]) * P, (c * PASSES + passes[-1] + 1) * P)
            nc.vector.quantize_mx(
                v_codes[:, cols].bitcast(FP8X4), v_scales[:, cols], v_bf[:].rearrange("s h e t -> s (h e t)"),
            )

        cast0 = placed("cast0", [P, T], BF16, AT_CAST)
        nc.scalar.activation(cast0[:, :HALF], left[:], ACT.Copy)
        nc.scalar.activation(cast0[:, HALF:], right[:], ACT.Copy)

        key_scales = keep.tile([P, I], U8, name="key_scales", align_bytes=64)
        nc.vector.tensor_copy(key_scales[:], scale_pool[:].indirect(offsets[:]))

        q_bf = keep.tile([P, Q, PACK], BF16, name="q_bf", align_bytes=64)
        nc.vector.tensor_copy(
            q_bf[:].rearrange("p (c i) t -> p c t i", i=4), q_raw[:].rearrange("p t (c i) -> p c t i", i=4),
        )
        q_codes = keep.tile([P, Q], U32, name="q_codes", align_bytes=64)
        q_scales = keep.tile([P, Q], U8, name="q_scales", align_bytes=64)
        nc.vector.quantize_mx(q_codes[:].bitcast(FP8X4), q_scales[:], q_bf[:].rearrange("p q t -> p (q t)"))

        scores = []
        for h in range(PASSES):
            key_words = placed("key_words%d" % h, [P, SLOTS], U32, AT_WORDS + h * 4 * SLOTS)
            nc.vector.tensor_copy(key_words[:], listed(word_pool[:].bitcast(U32), h * SLOTS, SLOTS))
            score = psum.tile([P, SLOTS], F32, name="score%d" % h)
            nc.tensor.matmul_mx(
                score[:], q_codes[:].bitcast(FP8X4), q_scales[:],
                key_words[:].bitcast(FP8X4), key_scales[:, h * SLOTS : (h + 1) * SLOTS],
                start=True, stop=True,
            )
            scores.append(score)

        best = placed("best", [P, G], F32, AT_BEST)
        for h in range(PASSES):
            nc.vector.tensor_reduce(
                best[:, h * (G // PASSES) : (h + 1) * (G // PASSES)],
                scores[h][:].rearrange("q (g j) -> q g j", j=16), AX.X, ALU.max,
            )
        neg_top = keep.tile([P, 1], F32, name="neg_top")
        nc.vector.tensor_reduce(neg_top[:], best[:], AX.X, ALU.max, negate=True)

        picked0 = placed("picked0", [P, I], BF16, AT_WORDS)
        for h in range(PASSES):
            nc.scalar.activation(picked0[:, h * SLOTS : (h + 1) * SLOTS], listed(cast0[:], h * SLOTS, SLOTS), ACT.Copy)

        share = placed("share", [P, G], F32, AT_CAST)
        share_sum = keep.tile([P, 1], F32, name="share_sum")
        nc.scalar.activation(share[:], best[:], ACT.Exp, bias=neg_top[:], accum_out=share_sum[:])
        prob = placed("prob", [P, PACK, PASSES, P], F32, AT_CAST + 4 * G)
        for h in range(PASSES):
            nc.scalar.activation(
                prob[:, :, h, :], scores[h][:].rearrange("q (s t) -> q t s", t=PACK), ACT.Exp, bias=neg_top[:],
            )

        v_scales = placed("v_scales", [P, PASSES * E], U8, AT_CAST + 4 * G + 2 * I)
        turn_and_quantise(0, (0, 1), picked0, keep.tile([P, PASSES, P, PACK], BF16, name="v_bf0", align_bytes=64))

        picked2 = placed("picked2", [P, I], BF16, AT_WORDS + 4 * SLOTS)
        for h in range(PASSES):
            nc.vector.tensor_copy(picked2[:, h * SLOTS : (h + 1) * SLOTS], listed(plane2[:], h * SLOTS, SLOTS))

        cast1 = placed("cast1", [P, T], BF16, AT_CAST1)
        nc.vector.tensor_copy(cast1[:, :HALF], plane1[:, :HALF])
        nc.scalar.activation(cast1[:, HALF:], plane1[:, HALF:], ACT.Copy)

        z = placed("z", [P, G], F32, AT_THIRD)
        nc.vector.tensor_reduce(z[:], prob[:].rearrange("q t h (g j) -> q (h g) t j", j=PACK), AX.XY, ALU.add)
        denom = keep.tile([P, G], F32, name="denom")
        nc.vector.tensor_scalar(denom[:], z[:], TINY, share_sum[:], ALU.max, ALU.mult)
        inv = keep.tile([P, G], F32, name="inv")
        nc.vector.reciprocal(inv[:], denom[:])
        factor = keep.tile([P, G, PACK], F32, name="factor")
        nc.vector.tensor_tensor(
            factor[:], share[:].unsqueeze(2).to_broadcast([P, G, PACK]), inv[:].unsqueeze(2).to_broadcast([P, G, PACK]), ALU.mult,
        )

        sized = []
        for h in range(PASSES):
            prob_t = psum.tile([P, PACK, Q], F32, name="prob_t%d" % h)
            for t in range(PACK):
                nc.tensor.transpose(prob_t[:, t, :], prob[:, t, h, :], ident[:])
            sized_h = keep.tile([P, PACK, Q], F32, name="sized%d" % h)
            for t in range(PACK):
                nc.scalar.activation(sized_h[:, t, :], prob_t[:, t, :], ACT.Copy, scale=size_cols[:, h, t : t + 1])
            sized.append(sized_h)

        factor_t = psum.tile([P, PASSES, Q], F32, name="factor_t")
        factor_cols = factor[:].rearrange("q (h g) j -> q h (g j)", h=PASSES)
        for h in range(PASSES):
            nc.tensor.transpose(factor_t[:, h, :], factor_cols[:, h, :], ident[:])

        turn_and_quantise(2, (0, 1), picked2, keep.tile([P, PASSES, P, PACK], BF16, name="v_bf2", align_bytes=64))

        picked3 = placed("picked3", [P, I], BF16, AT_CAST + 4 * G)
        for h in range(PASSES):
            nc.vector.tensor_copy(picked3[:, h * SLOTS : (h + 1) * SLOTS], listed(plane3[:], h * SLOTS, SLOTS))

        w_codes = keep.tile([P, PASSES * Q], U32, name="w_codes", align_bytes=64)
        w_scales = keep.tile([P, PASSES * Q], U8, name="w_scales", align_bytes=64)
        for h in range(PASSES):
            w_bf = placed("w_bf%d" % h, [P, Q, PACK], BF16, AT_LOADS + 3 * PLANE_BYTES + h * 2 * SLOTS)
            nc.vector.tensor_tensor(
                w_bf[:].rearrange("s (c i) t -> s c t i", i=4),
                sized[h][:].rearrange("s t (c i) -> s c t i", i=4),
                factor_t[:, h, :].rearrange("s (c i) -> s c i", i=4).unsqueeze(2).to_broadcast([P, Q // 4, PACK, 4]),
                ALU.mult,
            )
            nc.vector.quantize_mx(
                w_codes[:, h * Q : (h + 1) * Q].bitcast(FP8X4), w_scales[:, h * Q : (h + 1) * Q],
                w_bf[:].rearrange("s q t -> s (q t)"),
            )

        picked1 = keep.tile([P, I], BF16, name="picked1", align_bytes=64)
        for h in range(PASSES):
            nc.scalar.activation(picked1[:, h * SLOTS : (h + 1) * SLOTS], listed(cast1[:], h * SLOTS, SLOTS), ACT.Copy)
            turn_and_quantise(1, (h,), picked1, keep.tile([P, 1, P, PACK], BF16, name="v_bf1_%d" % h, align_bytes=64))

        turn_and_quantise(3, (0, 1), picked3, placed("v_bf3", [P, PASSES, P, PACK], BF16, AT_CAST1))

        for b in range(2):
            acc = psum.tile([P, 2, P], F32, name="score%d" % b)
            for n in range(2):
                for h in range(PASSES):
                    cols = slice(((2 * b + n) * PASSES + h) * P, ((2 * b + n) * PASSES + h + 1) * P)
                    nc.tensor.matmul_mx(
                        acc[:, n, :], w_codes[:, h * Q : (h + 1) * Q].bitcast(FP8X4), w_scales[:, h * Q : (h + 1) * Q],
                        v_codes[:, cols].bitcast(FP8X4), v_scales[:, cols],
                        start=(h == 0), stop=(h == PASSES - 1),
                    )
            result = keep.tile([P, 2 * P], F32, name="result%d" % b)
            if b == 0:
                nc.scalar.copy(result[:], acc[:].rearrange("q n e -> q (n e)"))
                nc.scalar.dma_start(out[:, : 2 * P], result[:])
            else:
                nc.vector.tensor_copy(result[:], acc[:].rearrange("q n e -> q (n e)"))
                nc.sync.dma_start(out[:, 2 * P :], result[:])
